import numpy as np
import ml_dtypes


def mxq(x, axis, fmt="e4m3"):
    dtype, down = {"e4m3": (ml_dtypes.float8_e4m3fn, 7), "e5m2": (ml_dtypes.float8_e5m2, 14)}[fmt]
    v = np.moveaxis(np.asarray(x, np.float32).astype(ml_dtypes.bfloat16).astype(np.float64), axis, -1)
    blocks = v.reshape(v.shape[:-1] + (-1, 32))
    amax = np.abs(blocks).max(-1, keepdims=True)
    byte = np.maximum(np.where(amax > 0, np.frexp(amax)[1] - 1 + 127, 0) - down, 1)
    scale = np.exp2(byte - 127.0)
    codes = (blocks / scale).astype(np.float32).astype(dtype).astype(np.float64)
    return np.moveaxis((codes * scale).reshape(v.shape), -1, axis)


WIDE = False


def mx_kscale(k, group=512):
    if not WIDE:
        return np.ones(k)
    levels = np.array([18, -18])
    if group != 512:
        return np.exp2(np.random.permutation(np.resize(levels, k // group))).repeat(group)
    if k % 512:
        return np.exp2(np.random.permutation(np.resize(levels, k // 32))).repeat(32)
    a = np.empty((k // 512, 16))
    for p in range(k // 512):
        a[p, :8] = np.random.permutation(np.resize(levels, 8))
        for g in range(8):
            far = levels[np.abs(levels - a[p, g]) >= 10]
            a[p, g + 8] = far[np.random.randint(len(far))]
    return np.exp2(a.ravel()).repeat(32)


def f64(x):
    return np.asarray(x).astype(np.float64)


G, D, M, N = 8, 128, 128, 512


def setup_inputs():
    n = np.random.standard_normal
    s = mx_kscale(D, 0)[:, None]
    return {
        "x": (n((G, D, N)) * s).astype(np.float32),
        "w": (n((G, D, M)) / np.sqrt(D) / s).astype(np.float32),
        "b": (0.5 * n((G, M, 1))).astype(np.float32),
        "r": n((G, M, N)).astype(np.float32),
    }


def reference(x, w, b, r):
    xq = mxq(f64(x), 1, "e4m3")
    y = mxq(f64(w), 1, "e4m3").transpose(0, 2, 1) @ xq
    y = y + f64(b)
    y = np.square(np.maximum(y, 0.0))
    y = y + f64(r)
    return y

@@ -1,0 +1,124 @@
+from contextlib import ExitStack
+
+import concourse.mybir as mybir
+
+G, D, M, N = 8, 128, 128, 512
+FLOPS = 2 * G * D * M * N
+
+F32 = mybir.dt.float32
+BF16 = mybir.dt.bfloat16
+U32 = mybir.dt.uint32
+U8 = mybir.dt.uint8
+FP8X4 = mybir.dt.float8_e4m3fn_x4
+ACT = mybir.ActivationFunctionType
+ALU = mybir.AluOpType
+
+P = 128
+PACK = 4
+ROWS = D // PACK
+SIDE = P // ROWS
+SETS = G // SIDE
+QUAD = 32
+R_PER_LOAD = 2
+
+
+def tile_rows_glin_relu2_bias_res_kernel(tc, x, w, b, r, out):
+    nc = tc.nc
+    with ExitStack() as ctx:
+        sb = ctx.enter_context(tc.tile_pool(name="sb", bufs=1))
+        ps = ctx.enter_context(tc.psum_pool(name="ps", bufs=1))
+        ctx.enter_context(tc.manual_schedule())
+
+        def tiles(name, count, shape, dtype):
+            return [sb.tile(shape, dtype, name="%s%d" % (name, i), align_bytes=64) for i in range(count)]
+
+        x_raw = tiles("x_raw", SETS, [P, PACK, N], F32)
+        w_raw = tiles("w_raw", SETS, [P, PACK, M], F32)
+        x_bf = tiles("x_bf", SETS, [P, N, PACK], BF16)
+        w_bf = tiles("w_bf", SETS, [P, M, PACK], BF16)
+        x_codes = tiles("x_codes", SETS, [P, N], U32)
+        w_codes = tiles("w_codes", SETS, [P, M], U32)
+        x_scales = tiles("x_scales", SETS, [P, N], U8)
+        w_scales = tiles("w_scales", SETS, [P, M], U8)
+        r_sb = tiles("r_sb", G // R_PER_LOAD, [P, R_PER_LOAD, N], F32)
+        rect = tiles("rect", G, [M, N], F32)
+        squared = tiles("squared", G, [M, N], F32)
+        result = tiles("result", G, [M, N], F32)
+        b_rows = sb.tile([P, G * QUAD], F32, align_bytes=64)
+        b_cols = sb.tile([P, G * QUAD], F32, align_bytes=64)
+        sums = [ps.tile([M, N], F32, name="sums%d" % g) for g in range(G)]
+
+        def load_rows(dst, src, s):
+            nc.sync.dma_start(out=dst[s][:], in_=src[SIDE * s : SIDE * (s + 1)].rearrange("g (p j) c -> (g p) j c", j=PACK))
+
+        def interleave(engine_copy, dst, src):
+            engine_copy(out=dst[:], in_=src[:].rearrange("p j c -> p c j"))
+
+        def quantize(codes, scales, src):
+            nc.vector.quantize_mx(out=codes[:].bitcast(FP8X4), scales=scales[:], in_=src[:].rearrange("p c j -> p (c j)"))
+
+        def multiply(s):
+            for c in range(SIDE):
+                rows = slice(ROWS * c, ROWS * (c + 1))
+                nc.tensor.matmul_mx(
+                    out=sums[SIDE * s + c][:],
+                    lhsT=w_codes[s][rows, :].bitcast(FP8X4),
+                    lhsT_scale=w_scales[s][rows, :],
+                    rhs=x_codes[s][rows, :].bitcast(FP8X4),
+                    rhs_scale=x_scales[s][rows, :],
+                    start=True,
+                    stop=True,
+                )
+
+        def bias(g):
+            return b_cols[:, QUAD * g : QUAD * g + 1]
+
+        def relu_scalar(g):
+            nc.scalar.activation(out=rect[g][:], in_=sums[g][:], func=ACT.Relu, bias=bias(g))
+
+        def relu_vector(g):
+            nc.vector.tensor_scalar(out=rect[g][:], in0=sums[g][:], scalar1=bias(g), scalar2=0.0, op0=ALU.add, op1=ALU.max)
+
+        def square(g):
+            nc.scalar.activation(out=squared[g][:], in_=rect[g][:], func=ACT.Square)
+
+        def add_and_store(g):
+            nc.vector.tensor_tensor(out=result[g][:], in0=squared[g][:], in1=r_sb[g // R_PER_LOAD][:, g % R_PER_LOAD, :], op=ALU.add)
+            nc.sync.dma_start(out=out[g], in_=result[g][:])
+
+        nc.vector.memset(b_rows[:], 0.0)
+        nc.scalar.dma_start(
+            out=b_rows[0:P:QUAD, :].rearrange("q (g i) -> q g i", i=QUAD),
+            in_=b.rearrange("g (q i) o -> q g (i o)", i=QUAD),
+        )
+        for s in range(SETS):
+            load_rows(x_raw, x, s)
+            load_rows(w_raw, w, s)
+        for i in range(G // R_PER_LOAD):
+            nc.sync.dma_start(out=r_sb[i][:], in_=r[R_PER_LOAD * i : R_PER_LOAD * (i + 1)].rearrange("g m n -> m g n"))
+        nc.vector.transpose(out=b_cols[:], in_=b_rows[:])
+
+        interleave(nc.vector.tensor_copy, x_bf[0], x_raw[0])
+        interleave(nc.scalar.copy, w_bf[0], w_raw[0])
+        quantize(x_codes[0], x_scales[0], x_bf[0])
+        quantize(w_codes[0], w_scales[0], w_bf[0])
+        multiply(0)
+
+        interleave(nc.vector.tensor_copy, x_bf[1], x_raw[1])
+        interleave(nc.vector.tensor_copy, w_bf[1], w_raw[1])
+        quantize(x_codes[1], x_scales[1], x_bf[1])
+        quantize(w_codes[1], w_scales[1], w_bf[1])
+        multiply(1)
+
+        for g in range(6):
+            relu_scalar(g)
+            square(g)
+        for g in range(3):
+            add_and_store(g)
+        relu_vector(6)
+        add_and_store(3)
+        relu_vector(7)
+        square(6)
+        square(7)
+        for g in range(4, 8):
+            add_and_store(g)

@@ -20,6 +20,8 @@ SIDE = P // ROWS
 SETS = G // SIDE
 QUAD = 32
 R_PER_LOAD = 2
+X0_SPLIT = 336
+HALF = N // 2
 
 
 def tile_rows_glin_relu2_bias_res_kernel(tc, x, w, b, r, out):
@@ -48,14 +50,24 @@ def tile_rows_glin_relu2_bias_res_kernel(tc, x, w, b, r, out):
         b_cols = sb.tile([P, G * QUAD], F32, align_bytes=64)
         sums = [ps.tile([M, N], F32, name="sums%d" % g) for g in range(G)]
 
-        def load_rows(dst, src, s):
-            nc.sync.dma_start(out=dst[s][:], in_=src[SIDE * s : SIDE * (s + 1)].rearrange("g (p j) c -> (g p) j c", j=PACK))
+        def load_x(s, cols):
+            rows = x[SIDE * s : SIDE * (s + 1)].rearrange("g (p j) c -> (g p) j c", j=PACK)
+            nc.sync.dma_start(out=x_raw[s][:, :, cols], in_=rows[:, :, cols])
 
-        def interleave(engine_copy, dst, src):
-            engine_copy(out=dst[:], in_=src[:].rearrange("p j c -> p c j"))
+        def load_w(s):
+            nc.sync.dma_start(out=w_raw[s][:], in_=w[SIDE * s : SIDE * (s + 1)].rearrange("g (p j) c -> (g p) j c", j=PACK))
 
-        def quantize(codes, scales, src):
-            nc.vector.quantize_mx(out=codes[:].bitcast(FP8X4), scales=scales[:], in_=src[:].rearrange("p c j -> p (c j)"))
+        def load_r(i):
+            nc.sync.dma_start(out=r_sb[i][:], in_=r[R_PER_LOAD * i : R_PER_LOAD * (i + 1)].rearrange("g m n -> m g n"))
+
+        def interleave(engine_copy, dst, src, cols):
+            engine_copy(
+                out=dst[:, cols, :].rearrange("p (c i) j -> p c j i", i=4),
+                in_=src[:, :, cols].rearrange("p j (c i) -> p c j i", i=4),
+            )
+
+        def quantize(codes, scales, src, cols):
+            nc.vector.quantize_mx(out=codes[:, cols].bitcast(FP8X4), scales=scales[:, cols], in_=src[:, cols, :].rearrange("p c j -> p (c j)"))
 
         def multiply(s):
             for c in range(SIDE):
@@ -87,38 +99,54 @@ def tile_rows_glin_relu2_bias_res_kernel(tc, x, w, b, r, out):
             nc.sync.dma_start(out=out[g], in_=result[g][:])
 
         nc.vector.memset(b_rows[:], 0.0)
-        nc.scalar.dma_start(
+        load_x(0, slice(0, N))
+        nc.sync.dma_start(
             out=b_rows[0:P:QUAD, :].rearrange("q (g i) -> q g i", i=QUAD),
             in_=b.rearrange("g (q i) o -> q g (i o)", i=QUAD),
         )
-        for s in range(SETS):
-            load_rows(x_raw, x, s)
-            load_rows(w_raw, w, s)
-        for i in range(G // R_PER_LOAD):
-            nc.sync.dma_start(out=r_sb[i][:], in_=r[R_PER_LOAD * i : R_PER_LOAD * (i + 1)].rearrange("g m n -> m g n"))
-        nc.vector.transpose(out=b_cols[:], in_=b_rows[:])
-
-        interleave(nc.vector.tensor_copy, x_bf[0], x_raw[0])
-        interleave(nc.scalar.copy, w_bf[0], w_raw[0])
-        quantize(x_codes[0], x_scales[0], x_bf[0])
-        quantize(w_codes[0], w_scales[0], w_bf[0])
+        load_w(0)
+        load_w(1)
+        load_x(1, slice(0, HALF))
+        load_x(1, slice(HALF, N))
+        load_r(0)
+        load_r(1)
+        load_r(2)
+        load_r(3)
+        interleave(nc.vector.tensor_copy, x_bf[0], x_raw[0], slice(0, X0_SPLIT))
+        interleave(nc.scalar.copy, x_bf[0], x_raw[0], slice(X0_SPLIT, N))
+        interleave(nc.scalar.copy, w_bf[0], w_raw[0], slice(0, M))
+        quantize(x_codes[0], x_scales[0], x_bf[0], slice(0, N))
+        quantize(w_codes[0], w_scales[0], w_bf[0], slice(0, M))
         multiply(0)
-
-        interleave(nc.vector.tensor_copy, x_bf[1], x_raw[1])
-        interleave(nc.vector.tensor_copy, w_bf[1], w_raw[1])
-        quantize(x_codes[1], x_scales[1], x_bf[1])
-        quantize(w_codes[1], w_scales[1], w_bf[1])
+        nc.vector.transpose(out=b_cols[:], in_=b_rows[:])
+        interleave(nc.scalar.copy, w_bf[1], w_raw[1], slice(0, M))
+        quantize(w_codes[1], w_scales[1], w_bf[1], slice(0, M))
+        interleave(nc.vector.tensor_copy, x_bf[1], x_raw[1], slice(0, HALF))
+        relu_scalar(0)
+        relu_vector(1)
+        quantize(x_codes[1], x_scales[1], x_bf[1], slice(0, HALF))
+        interleave(nc.vector.tensor_copy, x_bf[1], x_raw[1], slice(HALF, N))
+        relu_scalar(2)
+        square(0)
+        quantize(x_codes[1], x_scales[1], x_bf[1], slice(HALF, N))
         multiply(1)
-
-        for g in range(6):
-            relu_scalar(g)
-            square(g)
-        for g in range(3):
-            add_and_store(g)
-        relu_vector(6)
+        relu_scalar(3)
+        square(1)
+        square(2)
+        square(3)
+        add_and_store(0)
+        add_and_store(1)
+        relu_vector(4)
+        add_and_store(2)
+        relu_vector(5)
         add_and_store(3)
-        relu_vector(7)
+        relu_scalar(6)
+        square(4)
+        add_and_store(4)
+        relu_scalar(7)
+        square(5)
+        add_and_store(5)
         square(6)
         square(7)
-        for g in range(4, 8):
-            add_and_store(g)
+        add_and_store(6)
+        add_and_store(7)

@@ -19,9 +19,9 @@ ROWS = D // PACK
 SIDE = P // ROWS
 SETS = G // SIDE
 QUAD = 32
-R_PER_LOAD = 2
-X0_SPLIT = 336
 HALF = N // 2
+N_MX = 128
+SHARE = 168
 
 
 def tile_rows_glin_relu2_bias_res_kernel(tc, x, w, b, r, out):
@@ -42,10 +42,10 @@ def tile_rows_glin_relu2_bias_res_kernel(tc, x, w, b, r, out):
         w_codes = tiles("w_codes", SETS, [P, M], U32)
         x_scales = tiles("x_scales", SETS, [P, N], U8)
         w_scales = tiles("w_scales", SETS, [P, M], U8)
-        r_sb = tiles("r_sb", G // R_PER_LOAD, [P, R_PER_LOAD, N], F32)
-        rect = tiles("rect", G, [M, N], F32)
-        squared = tiles("squared", G, [M, N], F32)
-        result = tiles("result", G, [M, N], F32)
+        r_sb = sb.tile([M, G, N], F32)
+        rect = sb.tile([M, G, N], F32)
+        squared = sb.tile([M, G, N], F32)
+        result = sb.tile([M, G, N], F32)
         b_rows = sb.tile([P, G * QUAD], F32, align_bytes=64)
         b_cols = sb.tile([P, G * QUAD], F32, align_bytes=64)
         sums = [ps.tile([M, N], F32, name="sums%d" % g) for g in range(G)]
@@ -57,8 +57,11 @@ def tile_rows_glin_relu2_bias_res_kernel(tc, x, w, b, r, out):
         def load_w(s):
             nc.sync.dma_start(out=w_raw[s][:], in_=w[SIDE * s : SIDE * (s + 1)].rearrange("g (p j) c -> (g p) j c", j=PACK))
 
-        def load_r(i):
-            nc.sync.dma_start(out=r_sb[i][:], in_=r[R_PER_LOAD * i : R_PER_LOAD * (i + 1)].rearrange("g m n -> m g n"))
+        def load_r(groups):
+            nc.sync.dma_start(out=r_sb[:, groups, :], in_=r[groups].rearrange("g m n -> m g n"))
+
+        def store(groups):
+            nc.sync.dma_start(out=out[groups].rearrange("g m n -> m g n"), in_=result[:, groups, :])
 
         def interleave(engine_copy, dst, src, cols):
             engine_copy(
@@ -69,15 +72,17 @@ def tile_rows_glin_relu2_bias_res_kernel(tc, x, w, b, r, out):
         def quantize(codes, scales, src, cols):
             nc.vector.quantize_mx(out=codes[:, cols].bitcast(FP8X4), scales=scales[:, cols], in_=src[:, cols, :].rearrange("p c j -> p (c j)"))
 
-        def multiply(s):
-            for c in range(SIDE):
-                rows = slice(ROWS * c, ROWS * (c + 1))
+        def multiply(g, cols):
+            s, c = divmod(g, SIDE)
+            rows = slice(ROWS * c, ROWS * (c + 1))
+            for n0 in range(cols.start, cols.stop, N_MX):
+                part = slice(n0, n0 + N_MX)
                 nc.tensor.matmul_mx(
-                    out=sums[SIDE * s + c][:],
+                    out=sums[g][:, part],
                     lhsT=w_codes[s][rows, :].bitcast(FP8X4),
                     lhsT_scale=w_scales[s][rows, :],
-                    rhs=x_codes[s][rows, :].bitcast(FP8X4),
-                    rhs_scale=x_scales[s][rows, :],
+                    rhs=x_codes[s][rows, part].bitcast(FP8X4),
+                    rhs_scale=x_scales[s][rows, part],
                     start=True,
                     stop=True,
                 )
@@ -85,68 +90,94 @@ def tile_rows_glin_relu2_bias_res_kernel(tc, x, w, b, r, out):
         def bias(g):
             return b_cols[:, QUAD * g : QUAD * g + 1]
 
-        def relu_scalar(g):
-            nc.scalar.activation(out=rect[g][:], in_=sums[g][:], func=ACT.Relu, bias=bias(g))
+        def relu_scalar(g, cols):
+            nc.scalar.activation(out=rect[:, g, cols], in_=sums[g][:, cols], func=ACT.Relu, bias=bias(g))
 
-        def relu_vector(g):
-            nc.vector.tensor_scalar(out=rect[g][:], in0=sums[g][:], scalar1=bias(g), scalar2=0.0, op0=ALU.add, op1=ALU.max)
+        def relu_vector(g, cols):
+            nc.vector.tensor_scalar(out=rect[:, g, cols], in0=sums[g][:, cols], scalar1=bias(g), scalar2=0.0, op0=ALU.add, op1=ALU.max)
 
-        def square(g):
-            nc.scalar.activation(out=squared[g][:], in_=rect[g][:], func=ACT.Square)
+        def square(g, cols):
+            nc.scalar.activation(out=squared[:, g, cols], in_=rect[:, g, cols], func=ACT.Square)
 
-        def add_and_store(g):
-            nc.vector.tensor_tensor(out=result[g][:], in0=squared[g][:], in1=r_sb[g // R_PER_LOAD][:, g % R_PER_LOAD, :], op=ALU.add)
-            nc.sync.dma_start(out=out[g], in_=result[g][:])
+        def add(engine, g, cols):
+            engine.tensor_tensor(out=result[:, g, cols], in0=squared[:, g, cols], in1=r_sb[:, g, cols], op=ALU.add)
 
         nc.vector.memset(b_rows[:], 0.0)
-        load_x(0, slice(0, N))
+        load_w(0)
+        load_x(0, slice(0, HALF))
         nc.sync.dma_start(
             out=b_rows[0:P:QUAD, :].rearrange("q (g i) -> q g i", i=QUAD),
             in_=b.rearrange("g (q i) o -> q g (i o)", i=QUAD),
         )
-        load_w(0)
-        load_w(1)
+        load_x(0, slice(HALF, N))
         load_x(1, slice(0, HALF))
+        load_w(1)
         load_x(1, slice(HALF, N))
-        load_r(0)
-        load_r(1)
-        load_r(2)
-        load_r(3)
-        interleave(nc.vector.tensor_copy, x_bf[0], x_raw[0], slice(0, X0_SPLIT))
-        interleave(nc.scalar.copy, x_bf[0], x_raw[0], slice(X0_SPLIT, N))
-        interleave(nc.scalar.copy, w_bf[0], w_raw[0], slice(0, M))
-        quantize(x_codes[0], x_scales[0], x_bf[0], slice(0, N))
+        load_r(slice(0, 2))
+        load_r(slice(2, 4))
+        load_r(slice(4, 8))
+        interleave(nc.vector.tensor_copy, w_bf[0], w_raw[0], slice(0, M))
+        interleave(nc.vector.tensor_copy, x_bf[0], x_raw[0], slice(0, 0 + SHARE))
+        interleave(nc.scalar.copy, x_bf[0], x_raw[0], slice(0 + SHARE, HALF))
         quantize(w_codes[0], w_scales[0], w_bf[0], slice(0, M))
-        multiply(0)
+        quantize(x_codes[0], x_scales[0], x_bf[0], slice(0, HALF))
+        multiply(0, slice(0, HALF))
+        multiply(1, slice(0, HALF))
+        multiply(2, slice(0, HALF))
+        multiply(3, slice(0, HALF))
         nc.vector.transpose(out=b_cols[:], in_=b_rows[:])
-        interleave(nc.scalar.copy, w_bf[1], w_raw[1], slice(0, M))
-        quantize(w_codes[1], w_scales[1], w_bf[1], slice(0, M))
+        interleave(nc.vector.tensor_copy, x_bf[0], x_raw[0], slice(HALF, HALF + SHARE))
+        interleave(nc.scalar.copy, x_bf[0], x_raw[0], slice(HALF + SHARE, N))
+        quantize(x_codes[0], x_scales[0], x_bf[0], slice(HALF, N))
+        relu_scalar(0, slice(0, HALF))
+        multiply(0, slice(HALF, N))
+        relu_scalar(1, slice(0, HALF))
+        multiply(1, slice(HALF, N))
+        relu_scalar(2, slice(0, HALF))
+        multiply(2, slice(HALF, N))
+        relu_scalar(3, slice(0, HALF))
+        multiply(3, slice(HALF, N))
         interleave(nc.vector.tensor_copy, x_bf[1], x_raw[1], slice(0, HALF))
-        relu_scalar(0)
-        relu_vector(1)
+        interleave(nc.vector.tensor_copy, w_bf[1], w_raw[1], slice(0, M))
         quantize(x_codes[1], x_scales[1], x_bf[1], slice(0, HALF))
+        relu_scalar(0, slice(HALF, N))
+        relu_scalar(1, slice(HALF, N))
+        relu_vector(2, slice(HALF, N))
+        quantize(w_codes[1], w_scales[1], w_bf[1], slice(0, M))
+        multiply(4, slice(0, HALF))
+        multiply(5, slice(0, HALF))
+        multiply(6, slice(0, HALF))
+        multiply(7, slice(0, HALF))
         interleave(nc.vector.tensor_copy, x_bf[1], x_raw[1], slice(HALF, N))
-        relu_scalar(2)
-        square(0)
+        relu_vector(3, slice(HALF, N))
         quantize(x_codes[1], x_scales[1], x_bf[1], slice(HALF, N))
-        multiply(1)
-        relu_scalar(3)
-        square(1)
-        square(2)
-        square(3)
-        add_and_store(0)
-        add_and_store(1)
-        relu_vector(4)
-        add_and_store(2)
-        relu_vector(5)
-        add_and_store(3)
-        relu_scalar(6)
-        square(4)
-        add_and_store(4)
-        relu_scalar(7)
-        square(5)
-        add_and_store(5)
-        square(6)
-        square(7)
-        add_and_store(6)
-        add_and_store(7)
+        multiply(4, slice(HALF, N))
+        multiply(5, slice(HALF, N))
+        multiply(6, slice(HALF, N))
+        multiply(7, slice(HALF, N))
+        square(0, slice(0, N))
+        square(1, slice(0, N))
+        square(2, slice(0, N))
+        square(3, slice(0, N))
+        add(nc.vector, 0, slice(0, N))
+        add(nc.vector, 1, slice(0, N))
+        store(slice(0, 2))
+        relu_scalar(4, slice(0, N))
+        relu_scalar(5, slice(0, N))
+        add(nc.vector, 2, slice(0, N))
+        add(nc.vector, 3, slice(0, N))
+        store(slice(2, 4))
+        square(4, slice(0, N))
+        relu_scalar(6, slice(0, N))
+        square(5, slice(0, N))
+        relu_vector(7, slice(0, N))
+        add(nc.vector, 4, slice(0, N))
+        store(slice(4, 5))
+        square(6, slice(0, N))
+        add(nc.vector, 5, slice(0, N))
+        store(slice(5, 6))
+        square(7, slice(0, N))
+        add(nc.vector, 6, slice(0, N))
+        store(slice(6, 7))
+        add(nc.vector, 7, slice(0, N))
+        store(slice(7, 8))

@@ -103,81 +103,78 @@ def tile_rows_glin_relu2_bias_res_kernel(tc, x, w, b, r, out):
             engine.tensor_tensor(out=result[:, g, cols], in0=squared[:, g, cols], in1=r_sb[:, g, cols], op=ALU.add)
 
         nc.vector.memset(b_rows[:], 0.0)
-        load_w(0)
         load_x(0, slice(0, HALF))
+        load_w(0)
         nc.sync.dma_start(
             out=b_rows[0:P:QUAD, :].rearrange("q (g i) -> q g i", i=QUAD),
             in_=b.rearrange("g (q i) o -> q g (i o)", i=QUAD),
         )
         load_x(0, slice(HALF, N))
-        load_x(1, slice(0, HALF))
         load_w(1)
+        load_x(1, slice(0, HALF))
         load_x(1, slice(HALF, N))
         load_r(slice(0, 2))
         load_r(slice(2, 4))
-        load_r(slice(4, 8))
-        interleave(nc.vector.tensor_copy, w_bf[0], w_raw[0], slice(0, M))
+        load_r(slice(4, 6))
+        load_r(slice(6, 8))
         interleave(nc.vector.tensor_copy, x_bf[0], x_raw[0], slice(0, 0 + SHARE))
         interleave(nc.scalar.copy, x_bf[0], x_raw[0], slice(0 + SHARE, HALF))
-        quantize(w_codes[0], w_scales[0], w_bf[0], slice(0, M))
+        interleave(nc.scalar.copy, w_bf[0], w_raw[0], slice(0, M))
+        nc.vector.transpose(out=b_cols[:], in_=b_rows[:])
         quantize(x_codes[0], x_scales[0], x_bf[0], slice(0, HALF))
+        quantize(w_codes[0], w_scales[0], w_bf[0], slice(0, M))
         multiply(0, slice(0, HALF))
-        multiply(1, slice(0, HALF))
         multiply(2, slice(0, HALF))
         multiply(3, slice(0, HALF))
-        nc.vector.transpose(out=b_cols[:], in_=b_rows[:])
+        multiply(1, slice(0, HALF))
         interleave(nc.vector.tensor_copy, x_bf[0], x_raw[0], slice(HALF, HALF + SHARE))
         interleave(nc.scalar.copy, x_bf[0], x_raw[0], slice(HALF + SHARE, N))
+        interleave(nc.vector.tensor_copy, w_bf[1], w_raw[1], slice(0, M))
         quantize(x_codes[0], x_scales[0], x_bf[0], slice(HALF, N))
         relu_scalar(0, slice(0, HALF))
-        multiply(0, slice(HALF, N))
-        relu_scalar(1, slice(0, HALF))
-        multiply(1, slice(HALF, N))
         relu_scalar(2, slice(0, HALF))
-        multiply(2, slice(HALF, N))
         relu_scalar(3, slice(0, HALF))
+        relu_vector(1, slice(0, HALF))
+        multiply(0, slice(HALF, N))
+        multiply(1, slice(HALF, N))
+        multiply(2, slice(HALF, N))
         multiply(3, slice(HALF, N))
-        interleave(nc.vector.tensor_copy, x_bf[1], x_raw[1], slice(0, HALF))
-        interleave(nc.vector.tensor_copy, w_bf[1], w_raw[1], slice(0, M))
-        quantize(x_codes[1], x_scales[1], x_bf[1], slice(0, HALF))
-        relu_scalar(0, slice(HALF, N))
-        relu_scalar(1, slice(HALF, N))
-        relu_vector(2, slice(HALF, N))
         quantize(w_codes[1], w_scales[1], w_bf[1], slice(0, M))
+        interleave(nc.vector.tensor_copy, x_bf[1], x_raw[1], slice(0, HALF))
+        relu_vector(1, slice(HALF, N))
+        relu_scalar(0, slice(HALF, N))
+        relu_scalar(2, slice(HALF, N))
+        relu_scalar(3, slice(HALF, N))
+        interleave(nc.vector.tensor_copy, x_bf[1], x_raw[1], slice(HALF, N))
+        quantize(x_codes[1], x_scales[1], x_bf[1], slice(0, HALF))
         multiply(4, slice(0, HALF))
-        multiply(5, slice(0, HALF))
         multiply(6, slice(0, HALF))
         multiply(7, slice(0, HALF))
-        interleave(nc.vector.tensor_copy, x_bf[1], x_raw[1], slice(HALF, N))
-        relu_vector(3, slice(HALF, N))
+        multiply(5, slice(0, HALF))
         quantize(x_codes[1], x_scales[1], x_bf[1], slice(HALF, N))
         multiply(4, slice(HALF, N))
-        multiply(5, slice(HALF, N))
         multiply(6, slice(HALF, N))
         multiply(7, slice(HALF, N))
-        square(0, slice(0, N))
-        square(1, slice(0, N))
-        square(2, slice(0, N))
-        square(3, slice(0, N))
-        add(nc.vector, 0, slice(0, N))
-        add(nc.vector, 1, slice(0, N))
+        multiply(5, slice(HALF, N))
+        square(slice(0, 2), slice(0, N))
+        square(slice(2, 4), slice(0, N))
+        add(nc.vector, slice(0, 2), slice(0, N))
         store(slice(0, 2))
         relu_scalar(4, slice(0, N))
-        relu_scalar(5, slice(0, N))
-        add(nc.vector, 2, slice(0, N))
-        add(nc.vector, 3, slice(0, N))
+        relu_scalar(6, slice(0, N))
+        add(nc.vector, slice(2, 4), slice(0, N))
         store(slice(2, 4))
         square(4, slice(0, N))
-        relu_scalar(6, slice(0, N))
-        square(5, slice(0, N))
-        relu_vector(7, slice(0, N))
+        relu_scalar(7, slice(0, N))
+        relu_vector(5, slice(0, N))
         add(nc.vector, 4, slice(0, N))
         store(slice(4, 5))
-        square(6, slice(0, N))
+        square(5, slice(0, N))
         add(nc.vector, 5, slice(0, N))
         store(slice(5, 6))
-        square(7, slice(0, N))
+        square(6, slice(0, N))
         add(nc.vector, 6, slice(0, N))
         store(slice(6, 7))
+        square(7, slice(0, N))
         add(nc.vector, 7, slice(0, N))
         store(slice(7, 8))

from contextlib import ExitStack

import concourse.mybir as mybir

G, D, M, N = 8, 128, 128, 512
FLOPS = 2 * G * D * M * N

F32 = mybir.dt.float32
BF16 = mybir.dt.bfloat16
U32 = mybir.dt.uint32
U8 = mybir.dt.uint8
FP8X4 = mybir.dt.float8_e4m3fn_x4
ACT = mybir.ActivationFunctionType
ALU = mybir.AluOpType

P = 128
PACK = 4
ROWS = D // PACK
SIDE = P // ROWS
SETS = G // SIDE
QUAD = 32
HALF = N // 2
N_MX = 128
SHARE = 168


def tile_rows_glin_relu2_bias_res_kernel(tc, x, w, b, r, out):
    nc = tc.nc
    with ExitStack() as ctx:
        sb = ctx.enter_context(tc.tile_pool(name="sb", bufs=1))
        ps = ctx.enter_context(tc.psum_pool(name="ps", bufs=1))
        ctx.enter_context(tc.manual_schedule())

        def tiles(name, count, shape, dtype):
            return [sb.tile(shape, dtype, name="%s%d" % (name, i), align_bytes=64) for i in range(count)]

        x_raw = tiles("x_raw", SETS, [P, PACK, N], F32)
        w_raw = tiles("w_raw", SETS, [P, PACK, M], F32)
        x_bf = tiles("x_bf", SETS, [P, N, PACK], BF16)
        w_bf = tiles("w_bf", SETS, [P, M, PACK], BF16)
        x_codes = tiles("x_codes", SETS, [P, N], U32)
        w_codes = tiles("w_codes", SETS, [P, M], U32)
        x_scales = tiles("x_scales", SETS, [P, N], U8)
        w_scales = tiles("w_scales", SETS, [P, M], U8)
        r_sb = sb.tile([M, G, N], F32)
        rect = sb.tile([M, G, N], F32)
        squared = sb.tile([M, G, N], F32)
        result = sb.tile([M, G, N], F32)
        b_rows = sb.tile([P, G * QUAD], F32, align_bytes=64)
        b_cols = sb.tile([P, G * QUAD], F32, align_bytes=64)
        sums = [ps.tile([M, N], F32, name="sums%d" % g) for g in range(G)]

        def load_x(s, cols):
            rows = x[SIDE * s : SIDE * (s + 1)].rearrange("g (p j) c -> (g p) j c", j=PACK)
            nc.sync.dma_start(out=x_raw[s][:, :, cols], in_=rows[:, :, cols])

        def load_w(s):
            nc.sync.dma_start(out=w_raw[s][:], in_=w[SIDE * s : SIDE * (s + 1)].rearrange("g (p j) c -> (g p) j c", j=PACK))

        def load_r(groups):
            nc.sync.dma_start(out=r_sb[:, groups, :], in_=r[groups].rearrange("g m n -> m g n"))

        def store(groups):
            nc.sync.dma_start(out=out[groups].rearrange("g m n -> m g n"), in_=result[:, groups, :])

        def interleave(engine_copy, dst, src, cols):
            engine_copy(
                out=dst[:, cols, :].rearrange("p (c i) j -> p c j i", i=4),
                in_=src[:, :, cols].rearrange("p j (c i) -> p c j i", i=4),
            )

        def quantize(codes, scales, src, cols):
            nc.vector.quantize_mx(out=codes[:, cols].bitcast(FP8X4), scales=scales[:, cols], in_=src[:, cols, :].rearrange("p c j -> p (c j)"))

        def multiply(g, cols):
            s, c = divmod(g, SIDE)
            rows = slice(ROWS * c, ROWS * (c + 1))
            for n0 in range(cols.start, cols.stop, N_MX):
                part = slice(n0, n0 + N_MX)
                nc.tensor.matmul_mx(
                    out=sums[g][:, part],
                    lhsT=w_codes[s][rows, :].bitcast(FP8X4),
                    lhsT_scale=w_scales[s][rows, :],
                    rhs=x_codes[s][rows, part].bitcast(FP8X4),
                    rhs_scale=x_scales[s][rows, part],
                    start=True,
                    stop=True,
                )

        def bias(g):
            return b_cols[:, QUAD * g : QUAD * g + 1]

        def relu_scalar(g, cols):
            nc.scalar.activation(out=rect[:, g, cols], in_=sums[g][:, cols], func=ACT.Relu, bias=bias(g))

        def relu_vector(g, cols):
            nc.vector.tensor_scalar(out=rect[:, g, cols], in0=sums[g][:, cols], scalar1=bias(g), scalar2=0.0, op0=ALU.add, op1=ALU.max)

        def square(g, cols):
            nc.scalar.activation(out=squared[:, g, cols], in_=rect[:, g, cols], func=ACT.Square)

        def add(engine, g, cols):
            engine.tensor_tensor(out=result[:, g, cols], in0=squared[:, g, cols], in1=r_sb[:, g, cols], op=ALU.add)

        nc.vector.memset(b_rows[:], 0.0)
        load_x(0, slice(0, HALF))
        load_w(0)
        nc.sync.dma_start(
            out=b_rows[0:P:QUAD, :].rearrange("q (g i) -> q g i", i=QUAD),
            in_=b.rearrange("g (q i) o -> q g (i o)", i=QUAD),
        )
        load_x(0, slice(HALF, N))
        load_w(1)
        load_x(1, slice(0, HALF))
        load_x(1, slice(HALF, N))
        load_r(slice(0, 2))
        load_r(slice(2, 4))
        load_r(slice(4, 6))
        load_r(slice(6, 8))
        interleave(nc.vector.tensor_copy, x_bf[0], x_raw[0], slice(0, 0 + SHARE))
        interleave(nc.scalar.copy, x_bf[0], x_raw[0], slice(0 + SHARE, HALF))
        interleave(nc.scalar.copy, w_bf[0], w_raw[0], slice(0, M))
        nc.vector.transpose(out=b_cols[:], in_=b_rows[:])
        quantize(x_codes[0], x_scales[0], x_bf[0], slice(0, HALF))
        quantize(w_codes[0], w_scales[0], w_bf[0], slice(0, M))
        multiply(0, slice(0, HALF))
        multiply(2, slice(0, HALF))
        multiply(3, slice(0, HALF))
        multiply(1, slice(0, HALF))
        interleave(nc.vector.tensor_copy, x_bf[0], x_raw[0], slice(HALF, HALF + SHARE))
        interleave(nc.scalar.copy, x_bf[0], x_raw[0], slice(HALF + SHARE, N))
        interleave(nc.vector.tensor_copy, w_bf[1], w_raw[1], slice(0, M))
        quantize(x_codes[0], x_scales[0], x_bf[0], slice(HALF, N))
        relu_scalar(0, slice(0, HALF))
        relu_scalar(2, slice(0, HALF))
        relu_scalar(3, slice(0, HALF))
        relu_vector(1, slice(0, HALF))
        multiply(0, slice(HALF, N))
        multiply(1, slice(HALF, N))
        multiply(2, slice(HALF, N))
        multiply(3, slice(HALF, N))
        quantize(w_codes[1], w_scales[1], w_bf[1], slice(0, M))
        interleave(nc.vector.tensor_copy, x_bf[1], x_raw[1], slice(0, HALF))
        relu_vector(1, slice(HALF, N))
        relu_scalar(0, slice(HALF, N))
        relu_scalar(2, slice(HALF, N))
        relu_scalar(3, slice(HALF, N))
        interleave(nc.vector.tensor_copy, x_bf[1], x_raw[1], slice(HALF, N))
        quantize(x_codes[1], x_scales[1], x_bf[1], slice(0, HALF))
        multiply(4, slice(0, HALF))
        multiply(6, slice(0, HALF))
        multiply(7, slice(0, HALF))
        multiply(5, slice(0, HALF))
        quantize(x_codes[1], x_scales[1], x_bf[1], slice(HALF, N))
        multiply(4, slice(HALF, N))
        multiply(6, slice(HALF, N))
        multiply(7, slice(HALF, N))
        multiply(5, slice(HALF, N))
        square(slice(0, 2), slice(0, N))
        square(slice(2, 4), slice(0, N))
        add(nc.vector, slice(0, 2), slice(0, N))
        store(slice(0, 2))
        relu_scalar(4, slice(0, N))
        relu_scalar(6, slice(0, N))
        add(nc.vector, slice(2, 4), slice(0, N))
        store(slice(2, 4))
        square(4, slice(0, N))
        relu_scalar(7, slice(0, N))
        relu_vector(5, slice(0, N))
        add(nc.vector, 4, slice(0, N))
        store(slice(4, 5))
        square(5, slice(0, N))
        add(nc.vector, 5, slice(0, N))
        store(slice(5, 6))
        square(6, slice(0, N))
        add(nc.vector, 6, slice(0, N))
        store(slice(6, 7))
        square(7, slice(0, N))
        add(nc.vector, 7, slice(0, N))
        store(slice(7, 8))
